import numpy as np
import ml_dtypes


def mxq(x, axis, fmt="e4m3"):
    dtype, down = {"e4m3": (ml_dtypes.float8_e4m3fn, 7), "e5m2": (ml_dtypes.float8_e5m2, 14)}[fmt]
    v = np.moveaxis(np.asarray(x, np.float32).astype(ml_dtypes.bfloat16).astype(np.float64), axis, -1)
    blocks = v.reshape(v.shape[:-1] + (-1, 32))
    amax = np.abs(blocks).max(-1, keepdims=True)
    byte = np.maximum(np.where(amax > 0, np.frexp(amax)[1] - 1 + 127, 0) - down, 1)
    scale = np.exp2(byte - 127.0)
    codes = (blocks / scale).astype(np.float32).astype(dtype).astype(np.float64)
    return np.moveaxis((codes * scale).reshape(v.shape), -1, axis)


WIDE = False


def mx_kscale(k):
    if not WIDE:
        return np.ones(k)
    levels = np.array([10, -10, 5, -5, 0])
    if k % 512:
        return np.exp2(np.random.permutation(np.resize(levels, k // 32))).repeat(32)
    a = np.empty((k // 512, 16))
    for p in range(k // 512):
        a[p, :8] = np.random.permutation(np.resize(levels, 8))
        for g in range(8):
            far = levels[np.abs(levels - a[p, g]) >= 10]
            a[p, g + 8] = far[np.random.randint(len(far))]
    return np.exp2(a.ravel()).repeat(32)


def f64(x):
    return np.asarray(x).astype(np.float64)


def striped(idx):
    return np.tile(idx.reshape(-1, 16).T, (8, 1)).astype(np.uint16)


def unstriped(offs):
    return offs[:16].T.reshape(-1).astype(np.int64)


def silu(v):
    return v / (1.0 + np.exp(-np.maximum(v, -700.0)))


K, T, E, C, H, N = 2048, 512, 2, 256, 1024, 256


def by_expert(wq, xq):
    return np.concatenate([wq[e].T @ xq[:, e * C:(e + 1) * C] for e in range(E)], axis=1)


def setup_inputs():
    n = np.random.standard_normal
    s = mx_kscale(K)[:, None]
    u = mx_kscale(H)
    return {
        "xT": (n((K, T)) * s).astype(np.float32),
        "w1": (n((E, K, H)) / np.sqrt(K) / s[None] * u[None, None, :]).astype(np.float32),
        "w2": (n((E, H, N)) / np.sqrt(H) / u[None, :, None]).astype(np.float32),
        "gate": np.tile(np.random.uniform(0.2, 1.0, E * C), (N, 1)).astype(np.float32),
        "offs": striped(np.random.permutation(T)[:E * C]),
    }


def reference(xT, w1, w2, gate, offs):
    idx = unstriped(offs)
    xq = mxq(f64(xT)[:, idx], 0, "e4m3")
    h = silu(by_expert(mxq(f64(w1), 1, "e4m3"), xq))
    y = by_expert(mxq(f64(w2), 1, "e4m3"), mxq(h, 0, "e4m3"))
    out = np.zeros((N, T))
    out[:, idx] = f64(gate) * y
    return out

@@ -1,0 +1,265 @@
+from contextlib import ExitStack
+
+import concourse.mybir as mybir
+
+K, T, E, C, H, N = 2048, 512, 2, 256, 1024, 256
+FLOPS = 2 * E * C * (K * H + H * N)
+
+F32 = mybir.dt.float32
+BF16 = mybir.dt.bfloat16
+U32 = mybir.dt.uint32
+U16 = mybir.dt.uint16
+U8 = mybir.dt.uint8
+FP8X4 = mybir.dt.float8_e4m3fn_x4
+MULT = mybir.AluOpType.mult
+SILU = mybir.ActivationFunctionType.Silu
+
+P = 128
+PACK = 4
+KP = P * PACK
+PASSES = K // KP
+HALVES = H // KP
+NB = N // P
+LIST = C // 16
+
+RAW_BUFS = 6
+V_X = 128
+V_W1 = 48
+V_LAST = 80
+V_W2 = 0
+
+
+def tile_routed_moe_kernel(tc, xT, w1, w2, gate, offs, out):
+    nc = tc.nc
+    x_rows = xT.rearrange("(s p j) t -> s p j t", p=P, j=PACK)
+    w1_rows = w1.rearrange("e (s p j) i -> e s p j i", p=P, j=PACK)
+    w2_rows = w2.rearrange("e (s p j) n -> e s p j n", p=P, j=PACK)
+
+    with ExitStack() as ctx:
+        keep = ctx.enter_context(tc.tile_pool(name="keep", bufs=1))
+        raw_pool = ctx.enter_context(tc.tile_pool(name="raw_pool", bufs=RAW_BUFS))
+        lay_pool = ctx.enter_context(tc.tile_pool(name="lay_pool", bufs=4))
+        h_pool = ctx.enter_context(tc.tile_pool(name="h_pool", bufs=2))
+        psum = ctx.enter_context(tc.psum_pool(name="psum", bufs=8))
+
+        offsets = keep.tile([P, T // 16], U16, name="offsets")
+        warm = keep.tile([P, 8], F32, name="warm")
+        x_words = keep.tile([P, PASSES, T], U32, name="x_words", align_bytes=64)
+        x_bytes = keep.tile([P, T], U8, name="x_bytes", align_bytes=64)
+        g_words = keep.tile([P, PASSES, T], U32, name="g_words", align_bytes=64)
+        g_bytes = keep.tile([P, T], U8, name="g_bytes", align_bytes=64)
+        gate_sb = keep.tile([P, T], F32, name="gate_sb")
+        windows = [keep.tile([P, T], F32, name=f"window{b}") for b in range(NB)]
+        w1_words = [[keep.tile([P, H], U32, name=f"w1_words{e}{s}", align_bytes=64) for s in range(PASSES)] for e in range(E)]
+        w1_bytes = [[keep.tile([P, H], U8, name=f"w1_bytes{e}{s}", align_bytes=64) for s in range(PASSES)] for e in range(E)]
+        w2_words = [[keep.tile([P, N], U32, name=f"w2_words{e}{s}", align_bytes=64) for s in range(HALVES)] for e in range(E)]
+        w2_bytes = [[keep.tile([P, N], U8, name=f"w2_bytes{e}{s}", align_bytes=64) for s in range(HALVES)] for e in range(E)]
+
+        nc.vector.memset(warm[:], 0.0)
+        nc.scalar.activation(warm[:], warm[:], SILU)
+        nc.gpsimd.memset(x_bytes[:], 0)
+
+        raws = {}
+
+        def load_x(pair):
+            raw = raw_pool.tile([P, 2, PACK, T], F32, name="raw", tag="raw")
+            raws["x", pair] = raw
+            for i in range(2):
+                nc.sync.dma_start(raw[:, i, :, :], x_rows[2 * pair + i])
+                if pair == 0 and i == 0:
+                    nc.sync.dma_start(offsets[:], offs)
+
+        def load_w1(e, s):
+            raw = raw_pool.tile([P, PACK, H], F32, name="raw", tag="raw")
+            raws["w1", e, s] = raw
+            if e == E - 1 and s == PASSES - 1:
+                for hh in range(HALVES):
+                    cols = slice(hh * KP, (hh + 1) * KP)
+                    nc.sync.dma_start(raw[:, :, cols], w1_rows[e, s, :, :, cols])
+            else:
+                nc.sync.dma_start(raw[:], w1_rows[e, s])
+
+        def load_w2(e):
+            raw = raw_pool.tile([P, HALVES, PACK, N], F32, name="raw", tag="raw")
+            raws["w2", e] = raw
+            for s in range(HALVES):
+                nc.sync.dma_start(raw[:, s, :, :], w2_rows[e, s])
+            if e == 0:
+                nc.sync.dma_start(gate_sb[:], gate[0:P, :])
+
+        loads = [lambda pair=pair: load_x(pair) for pair in range(2)]
+        for e in range(E):
+            loads += [lambda e=e, s=s: load_w1(e, s) for s in range(PASSES)]
+            loads += [lambda e=e: load_w2(e)]
+
+        def plain_lay(dst, src, cols, split):
+            for engine, c0, c1 in ((nc.vector.tensor_copy, 0, split), (nc.scalar.copy, split, cols)):
+                if c1 > c0:
+                    engine(
+                        dst[:, c0:c1, :].rearrange("p (c i) j -> p c j i", i=4),
+                        src[:, :, c0:c1].rearrange("p j (c i) -> p c j i", i=4),
+                    )
+
+        def w1_lay(dst, src, split):
+            for engine, m0, m1 in ((nc.vector.tensor_copy, 0, split), (nc.scalar.copy, split, P)):
+                if m1 > m0:
+                    engine(
+                        dst[:, :, m0:m1, :].rearrange("p t m j -> p m j t"),
+                        src[:, :, 4 * m0 : 4 * m1].rearrange("p j (m t) -> p m j t", t=4),
+                    )
+
+        accs = {}
+        h_codes = {}
+        y_banks = {}
+
+        def x_unit(s):
+            laid = lay_pool.tile([P, T, PACK], BF16, name="laid", tag="laid", align_bytes=64)
+
+            def lay():
+                plain_lay(laid, raws["x", s // 2][:, s % 2, :, :], T, V_X)
+
+            def finish():
+                nc.vector.quantize_mx(
+                    out=x_words[:, s, :].bitcast(FP8X4),
+                    scales=x_bytes[4 * s : P, :],
+                    in_=laid[:].rearrange("p c j -> p (c j)"),
+                )
+                if s == PASSES - 1:
+                    gather(0)
+
+            return lay, finish
+
+        def gather(e):
+            cols = slice(e * C, (e + 1) * C)
+            picked = offsets[:, e * LIST : (e + 1) * LIST]
+            nc.vector.tensor_copy(g_bytes[:, cols], x_bytes[:].indirect(picked))
+            for s in range(PASSES):
+                nc.vector.tensor_copy(g_words[:, s, cols], x_words[:, s, :].indirect(picked))
+
+        def w1_unit(e, s, hh):
+            laid = lay_pool.tile([P, 4, P, PACK], BF16, name="laid", tag="laid", align_bytes=64)
+            cols = slice(hh * KP, (hh + 1) * KP)
+            last = e == E - 1 and s == PASSES - 1
+
+            def lay():
+                w1_lay(laid, raws["w1", e, s][:, :, cols], V_LAST if last else V_W1)
+
+            def finish():
+                nc.vector.quantize_mx(
+                    out=w1_words[e][s][:, cols].bitcast(FP8X4),
+                    scales=w1_bytes[e][s][:, cols],
+                    in_=laid[:].rearrange("p t m j -> p (t m j)"),
+                )
+                for t in range(4):
+                    if s == 0:
+                        accs[e, hh, t] = psum.tile([P, C], F32, name="bank", tag="bank")
+                    block = slice(hh * KP + t * P, hh * KP + (t + 1) * P)
+                    nc.tensor.matmul_mx(
+                        out=accs[e, hh, t][:],
+                        lhsT=w1_words[e][s][:, block].bitcast(FP8X4),
+                        lhsT_scale=w1_bytes[e][s][:, block],
+                        rhs=g_words[:, s, e * C : (e + 1) * C].bitcast(FP8X4),
+                        rhs_scale=g_bytes[4 * s : P, e * C : (e + 1) * C],
+                        start=(s == 0),
+                        stop=(s == PASSES - 1),
+                    )
+                if e == 0 and s == 1 and hh == 1:
+                    gather(1)
+                if s == PASSES - 1:
+                    hidden(e, hh)
+
+            return lay, finish
+
+        def w2_unit(e, s):
+            laid = lay_pool.tile([P, N, PACK], BF16, name="laid", tag="laid", align_bytes=64)
+
+            def lay():
+                plain_lay(laid, raws["w2", e][:, s, :, :], N, V_W2)
+
+            def finish():
+                nc.vector.quantize_mx(
+                    out=w2_words[e][s][:].bitcast(FP8X4),
+                    scales=w2_bytes[e][s][:],
+                    in_=laid[:].rearrange("p c j -> p (c j)"),
+                )
+                layer2(e, s)
+
+            return lay, finish
+
+        def chunks(e):
+            width = C if e == 0 else P
+            return [slice(c, c + width) for c in range(0, C, width)]
+
+        def hidden(e, hh):
+            h_flat = h_pool.tile([P, 4, C], BF16, name="h_flat", tag="h_flat", align_bytes=64)
+            h_laid = h_pool.tile([P, C, PACK], BF16, name="h_laid", tag="h_laid", align_bytes=64)
+            words = h_pool.tile([P, C], U32, name="h_words", tag=f"h_words{hh}", align_bytes=64)
+            scales = h_pool.tile([P, C], U8, name="h_bytes", tag=f"h_bytes{hh}", align_bytes=64)
+            h_codes[e, hh] = (words, scales)
+            for chunk in chunks(e) if hh == HALVES - 1 else [slice(0, C)]:
+                for t in range(4):
+                    nc.scalar.activation(h_flat[:, t, chunk], accs[e, hh, t][:, chunk], SILU)
+                nc.vector.tensor_copy(
+                    h_laid[:, chunk, :].rearrange("p (c i) t -> p c t i", i=4),
+                    h_flat[:, :, chunk].rearrange("p t (c i) -> p c t i", i=4),
+                )
+                nc.vector.quantize_mx(
+                    out=words[:, chunk].bitcast(FP8X4),
+                    scales=scales[:, chunk],
+                    in_=h_laid[:, chunk, :].rearrange("p c t -> p (c t)"),
+                )
+
+        def layer2(e, s):
+            for c, chunk in enumerate(chunks(e)):
+                width = chunk.stop - chunk.start
+                words, scales = h_codes[e, s]
+                for b in range(NB):
+                    if s == 0:
+                        y_banks[e, c, b] = psum.tile([P, width], F32, name="bank", tag="bank")
+                    n_cols = slice(b * P, (b + 1) * P)
+                    nc.tensor.matmul_mx(
+                        out=y_banks[e, c, b][:],
+                        lhsT=w2_words[e][s][:, n_cols].bitcast(FP8X4),
+                        lhsT_scale=w2_bytes[e][s][:, n_cols],
+                        rhs=words[:, chunk].bitcast(FP8X4),
+                        rhs_scale=scales[:, chunk],
+                        start=(s == 0),
+                        stop=(s == HALVES - 1),
+                    )
+                if s == HALVES - 1:
+                    first = e * C + chunk.start
+                    for b in range(NB):
+                        y_sb = h_pool.tile([P, width], F32, name="y_sb", tag=f"y_sb{b}")
+                        nc.scalar.copy(y_sb[:], y_banks[e, c, b][:])
+                        nc.vector.tensor_tensor(
+                            windows[b][:].indirect(offsets[:, first // 16 : (first + width) // 16]),
+                            y_sb[:],
+                            gate_sb[:, first : first + width],
+                            MULT,
+                        )
+
+        steps = []
+        for s in range(PASSES):
+            steps.append((s // 2, lambda s=s: x_unit(s)))
+        for e in range(E):
+            for s in range(PASSES):
+                for hh in range(HALVES):
+                    steps.append((2 + e * 5 + s, lambda e=e, s=s, hh=hh: w1_unit(e, s, hh)))
+            for s in range(HALVES):
+                steps.append((2 + e * 5 + 4, lambda e=e, s=s: w2_unit(e, s)))
+
+        loaded = 0
+        waiting = None
+        for tile_index, make in steps:
+            while loaded < len(loads) and loaded < tile_index + RAW_BUFS:
+                loads[loaded]()
+                loaded += 1
+            lay, finish = make()
+            lay()
+            if waiting is not None:
+                waiting()
+            waiting = finish
+        waiting()
+
+        for b in range(NB):
+            nc.sync.dma_start(out[b * P : (b + 1) * P, :], windows[b][:])

@@ -24,9 +24,9 @@ LIST = C // 16
 
 RAW_BUFS = 6
 V_X = 128
-V_W1 = 48
-V_LAST = 80
-V_W2 = 0
+V_W1 = {(0, 0): 48, (0, 1): 48, (0, 2): 48, (0, 3): 48, (1, 0): 56, (1, 1): 56, (1, 2): 64, (1, 3): 64}
+V_LAST = 72
+V_W2 = {(0, 0): 0, (0, 1): 0, (1, 0): 128, (1, 1): 128}
 
 
 def tile_routed_moe_kernel(tc, xT, w1, w2, gate, offs, out):
@@ -44,222 +44,294 @@ def tile_routed_moe_kernel(tc, xT, w1, w2, gate, offs, out):
 
         offsets = keep.tile([P, T // 16], U16, name="offsets")
         warm = keep.tile([P, 8], F32, name="warm")
+        ones = keep.tile([P, P], F32, name="ones")
+        gate_row = keep.tile([P, T], F32, name="gate_row")
+        gate_sb = keep.tile([P, T], F32, name="gate_sb")
         x_words = keep.tile([P, PASSES, T], U32, name="x_words", align_bytes=64)
         x_bytes = keep.tile([P, T], U8, name="x_bytes", align_bytes=64)
         g_words = keep.tile([P, PASSES, T], U32, name="g_words", align_bytes=64)
         g_bytes = keep.tile([P, T], U8, name="g_bytes", align_bytes=64)
-        gate_sb = keep.tile([P, T], F32, name="gate_sb")
         windows = [keep.tile([P, T], F32, name=f"window{b}") for b in range(NB)]
-        w1_words = [[keep.tile([P, H], U32, name=f"w1_words{e}{s}", align_bytes=64) for s in range(PASSES)] for e in range(E)]
-        w1_bytes = [[keep.tile([P, H], U8, name=f"w1_bytes{e}{s}", align_bytes=64) for s in range(PASSES)] for e in range(E)]
-        w2_words = [[keep.tile([P, N], U32, name=f"w2_words{e}{s}", align_bytes=64) for s in range(HALVES)] for e in range(E)]
-        w2_bytes = [[keep.tile([P, N], U8, name=f"w2_bytes{e}{s}", align_bytes=64) for s in range(HALVES)] for e in range(E)]
+        w1_words = {}
+        w1_bytes = {}
+        w2_words = {}
+        w2_bytes = {}
+        for e in range(E):
+            for s in range(PASSES):
+                w1_words[e, s] = keep.tile([P, H], U32, name=f"w1_words{e}{s}", align_bytes=64)
+                w1_bytes[e, s] = keep.tile([P, H], U8, name=f"w1_bytes{e}{s}", align_bytes=64)
+            for s in range(HALVES):
+                w2_words[e, s] = keep.tile([P, N], U32, name=f"w2_words{e}{s}", align_bytes=64)
+                w2_bytes[e, s] = keep.tile([P, N], U8, name=f"w2_bytes{e}{s}", align_bytes=64)
 
         nc.vector.memset(warm[:], 0.0)
         nc.scalar.activation(warm[:], warm[:], SILU)
         nc.gpsimd.memset(x_bytes[:], 0)
+        nc.gpsimd.memset(gate_row[:], 0.0)
+        nc.gpsimd.memset(ones[:], 1.0)
 
         raws = {}
-
-        def load_x(pair):
-            raw = raw_pool.tile([P, 2, PACK, T], F32, name="raw", tag="raw")
-            raws["x", pair] = raw
-            for i in range(2):
-                nc.sync.dma_start(raw[:, i, :, :], x_rows[2 * pair + i])
-                if pair == 0 and i == 0:
-                    nc.sync.dma_start(offsets[:], offs)
-
-        def load_w1(e, s):
-            raw = raw_pool.tile([P, PACK, H], F32, name="raw", tag="raw")
-            raws["w1", e, s] = raw
-            if e == E - 1 and s == PASSES - 1:
-                for hh in range(HALVES):
-                    cols = slice(hh * KP, (hh + 1) * KP)
-                    nc.sync.dma_start(raw[:, :, cols], w1_rows[e, s, :, :, cols])
-            else:
-                nc.sync.dma_start(raw[:], w1_rows[e, s])
-
-        def load_w2(e):
-            raw = raw_pool.tile([P, HALVES, PACK, N], F32, name="raw", tag="raw")
-            raws["w2", e] = raw
-            for s in range(HALVES):
-                nc.sync.dma_start(raw[:, s, :, :], w2_rows[e, s])
-            if e == 0:
-                nc.sync.dma_start(gate_sb[:], gate[0:P, :])
-
-        loads = [lambda pair=pair: load_x(pair) for pair in range(2)]
-        for e in range(E):
-            loads += [lambda e=e, s=s: load_w1(e, s) for s in range(PASSES)]
-            loads += [lambda e=e: load_w2(e)]
-
-        def plain_lay(dst, src, cols, split):
-            for engine, c0, c1 in ((nc.vector.tensor_copy, 0, split), (nc.scalar.copy, split, cols)):
-                if c1 > c0:
-                    engine(
-                        dst[:, c0:c1, :].rearrange("p (c i) j -> p c j i", i=4),
-                        src[:, :, c0:c1].rearrange("p j (c i) -> p c j i", i=4),
-                    )
-
-        def w1_lay(dst, src, split):
-            for engine, m0, m1 in ((nc.vector.tensor_copy, 0, split), (nc.scalar.copy, split, P)):
-                if m1 > m0:
-                    engine(
-                        dst[:, :, m0:m1, :].rearrange("p t m j -> p m j t"),
-                        src[:, :, 4 * m0 : 4 * m1].rearrange("p j (m t) -> p m j t", t=4),
-                    )
-
+        laid = {}
         accs = {}
         h_codes = {}
+        h_stage = {}
         y_banks = {}
 
-        def x_unit(s):
-            laid = lay_pool.tile([P, T, PACK], BF16, name="laid", tag="laid", align_bytes=64)
+        def load(item):
+            kind = item[0]
+            if kind == "x":
+                raw = raw_pool.tile([P, 2, PACK, T], F32, name="raw", tag="raw")
+                for i in range(2):
+                    nc.sync.dma_start(raw[:, i, :, :], x_rows[2 * item[1] + i])
+                    if item[1] == 0 and i == 0:
+                        nc.sync.dma_start(offsets[:], offs)
+                        nc.sync.dma_start(gate_row[0:1, :], gate[0:1, :])
+            elif kind == "w1":
+                e, s = item[1:]
+                raw = raw_pool.tile([P, PACK, H], F32, name="raw", tag="raw")
+                if e == E - 1 and s == PASSES - 1:
+                    nc.sync.dma_start(raw[:, :, 0:KP], w1_rows[e, s, :, :, 0:KP])
+                    for j in range(0, PACK, 2):
+                        nc.sync.dma_start(raw[:, j : j + 2, KP:H], w1_rows[e, s, :, j : j + 2, KP:H])
+                else:
+                    nc.sync.dma_start(raw[:], w1_rows[e, s])
+            else:
+                e = item[1]
+                raw = raw_pool.tile([P, HALVES, PACK, N], F32, name="raw", tag="raw")
+                for s in range(HALVES):
+                    nc.sync.dma_start(raw[:, s, :, :], w2_rows[e, s])
+            raws[item] = raw
 
-            def lay():
-                plain_lay(laid, raws["x", s // 2][:, s % 2, :, :], T, V_X)
-
-            def finish():
-                nc.vector.quantize_mx(
-                    out=x_words[:, s, :].bitcast(FP8X4),
-                    scales=x_bytes[4 * s : P, :],
-                    in_=laid[:].rearrange("p c j -> p (c j)"),
+        def lay_plain(dst, src, columns, split):
+            if split > 0:
+                nc.vector.tensor_copy(
+                    dst[:, 0:split, :].rearrange("p (c i) j -> p c j i", i=4),
+                    src[:, :, 0:split].rearrange("p j (c i) -> p c j i", i=4),
                 )
-                if s == PASSES - 1:
-                    gather(0)
+            if split < columns:
+                nc.scalar.copy(
+                    dst[:, split:columns, :].rearrange("p (c i) j -> p c j i", i=4),
+                    src[:, :, split:columns].rearrange("p j (c i) -> p c j i", i=4),
+                )
 
-            return lay, finish
+        def lay_blocks(dst, src, split, js):
+            for j in range(0, PACK, js):
+                if split > 0:
+                    nc.vector.tensor_copy(
+                        dst[:, :, 0:split, j : j + js].rearrange("p t m j -> p m j t"),
+                        src[:, j : j + js, 0 : 4 * split].rearrange("p j (m t) -> p m j t", t=4),
+                    )
+                if split < P:
+                    nc.scalar.copy(
+                        dst[:, :, split:P, j : j + js].rearrange("p t m j -> p m j t"),
+                        src[:, j : j + js, 4 * split : KP].rearrange("p j (m t) -> p m j t", t=4),
+                    )
+
+        def lay(unit):
+            kind = unit[0]
+            if kind == "x":
+                s = unit[1]
+                tile = lay_pool.tile([P, T, PACK], BF16, name="laid", tag="laid", align_bytes=64)
+                lay_plain(tile, raws["x", s // 2][:, s % 2, :, :], T, V_X)
+            elif kind == "w1":
+                e, s, half = unit[1:]
+                tile = lay_pool.tile([P, 4, P, PACK], BF16, name="laid", tag="laid", align_bytes=64)
+                last = e == E - 1 and s == PASSES - 1 and half == HALVES - 1
+                lay_blocks(tile, raws["w1", e, s][:, :, half * KP : (half + 1) * KP], V_LAST if last else V_W1[e, s], 2 if last else PACK)
+            else:
+                e, s = unit[1:]
+                tile = lay_pool.tile([P, N, PACK], BF16, name="laid", tag="laid", align_bytes=64)
+                lay_plain(tile, raws["w2", e][:, s, :, :], N, V_W2[e, s])
+            laid[unit] = tile
+
+        def finish_x(s):
+            nc.vector.quantize_mx(
+                out=x_words[:, s, :].bitcast(FP8X4),
+                scales=x_bytes[4 * s : P, :],
+                in_=laid["x", s][:].rearrange("p c j -> p (c j)"),
+            )
+
+        def broadcast_gate():
+            bank = psum.tile([P, T], F32, name="bank", tag="bank")
+            nc.tensor.matmul(bank[:], ones[:], gate_row[:], start=True, stop=True)
+            nc.scalar.copy(gate_sb[:], bank[:])
 
         def gather(e):
-            cols = slice(e * C, (e + 1) * C)
+            columns = slice(e * C, (e + 1) * C)
             picked = offsets[:, e * LIST : (e + 1) * LIST]
-            nc.vector.tensor_copy(g_bytes[:, cols], x_bytes[:].indirect(picked))
+            nc.vector.tensor_copy(g_bytes[:, columns], x_bytes[:].indirect(picked))
             for s in range(PASSES):
-                nc.vector.tensor_copy(g_words[:, s, cols], x_words[:, s, :].indirect(picked))
+                nc.vector.tensor_copy(g_words[:, s, columns], x_words[:, s, :].indirect(picked))
 
-        def w1_unit(e, s, hh):
-            laid = lay_pool.tile([P, 4, P, PACK], BF16, name="laid", tag="laid", align_bytes=64)
-            cols = slice(hh * KP, (hh + 1) * KP)
-            last = e == E - 1 and s == PASSES - 1
-
-            def lay():
-                w1_lay(laid, raws["w1", e, s][:, :, cols], V_LAST if last else V_W1)
-
-            def finish():
+        def quant_w1(e, s, half):
+            pieces = (4 if half == HALVES - 1 else 1) if e == E - 1 and s == PASSES - 1 else 1
+            for q in range(pieces):
+                blocks = slice(q * 4 // pieces, (q + 1) * 4 // pieces)
+                columns = slice(half * KP + blocks.start * P, half * KP + blocks.stop * P)
                 nc.vector.quantize_mx(
-                    out=w1_words[e][s][:, cols].bitcast(FP8X4),
-                    scales=w1_bytes[e][s][:, cols],
-                    in_=laid[:].rearrange("p t m j -> p (t m j)"),
+                    out=w1_words[e, s][:, columns].bitcast(FP8X4),
+                    scales=w1_bytes[e, s][:, columns],
+                    in_=laid["w1", e, s, half][:, blocks, :, :].rearrange("p t m j -> p (t m j)"),
                 )
+
+        def layer1(e, s, half):
+            parts = 1
+            for n in range(parts):
+                n_cols = slice(n * C // parts, (n + 1) * C // parts)
+                g_cols = slice(e * C + n_cols.start, e * C + n_cols.stop)
                 for t in range(4):
                     if s == 0:
-                        accs[e, hh, t] = psum.tile([P, C], F32, name="bank", tag="bank")
-                    block = slice(hh * KP + t * P, hh * KP + (t + 1) * P)
+                        accs[e, half, t] = psum.tile([P, C], F32, name="bank", tag="bank")
+                    block = slice(half * KP + t * P, half * KP + (t + 1) * P)
                     nc.tensor.matmul_mx(
-                        out=accs[e, hh, t][:],
-                        lhsT=w1_words[e][s][:, block].bitcast(FP8X4),
-                        lhsT_scale=w1_bytes[e][s][:, block],
-                        rhs=g_words[:, s, e * C : (e + 1) * C].bitcast(FP8X4),
-                        rhs_scale=g_bytes[4 * s : P, e * C : (e + 1) * C],
+                        out=accs[e, half, t][:, n_cols],
+                        lhsT=w1_words[e, s][:, block].bitcast(FP8X4),
+                        lhsT_scale=w1_bytes[e, s][:, block],
+                        rhs=g_words[:, s, g_cols].bitcast(FP8X4),
+                        rhs_scale=g_bytes[4 * s : P, g_cols],
                         start=(s == 0),
                         stop=(s == PASSES - 1),
                     )
-                if e == 0 and s == 1 and hh == 1:
-                    gather(1)
-                if s == PASSES - 1:
-                    hidden(e, hh)
-
-            return lay, finish
-
-        def w2_unit(e, s):
-            laid = lay_pool.tile([P, N, PACK], BF16, name="laid", tag="laid", align_bytes=64)
-
-            def lay():
-                plain_lay(laid, raws["w2", e][:, s, :, :], N, V_W2)
-
-            def finish():
-                nc.vector.quantize_mx(
-                    out=w2_words[e][s][:].bitcast(FP8X4),
-                    scales=w2_bytes[e][s][:],
-                    in_=laid[:].rearrange("p c j -> p (c j)"),
-                )
-                layer2(e, s)
-
-            return lay, finish
 
         def chunks(e):
-            width = C if e == 0 else P
+            width = C if e == 0 else 128
             return [slice(c, c + width) for c in range(0, C, width)]
 
-        def hidden(e, hh):
-            h_flat = h_pool.tile([P, 4, C], BF16, name="h_flat", tag="h_flat", align_bytes=64)
-            h_laid = h_pool.tile([P, C, PACK], BF16, name="h_laid", tag="h_laid", align_bytes=64)
-            words = h_pool.tile([P, C], U32, name="h_words", tag=f"h_words{hh}", align_bytes=64)
-            scales = h_pool.tile([P, C], U8, name="h_bytes", tag=f"h_bytes{hh}", align_bytes=64)
-            h_codes[e, hh] = (words, scales)
-            for chunk in chunks(e) if hh == HALVES - 1 else [slice(0, C)]:
-                for t in range(4):
-                    nc.scalar.activation(h_flat[:, t, chunk], accs[e, hh, t][:, chunk], SILU)
-                nc.vector.tensor_copy(
-                    h_laid[:, chunk, :].rearrange("p (c i) t -> p c t i", i=4),
-                    h_flat[:, :, chunk].rearrange("p t (c i) -> p c t i", i=4),
-                )
-                nc.vector.quantize_mx(
-                    out=words[:, chunk].bitcast(FP8X4),
-                    scales=scales[:, chunk],
-                    in_=h_laid[:, chunk, :].rearrange("p c t -> p (c t)"),
-                )
+        def hidden(e, half):
+            start_hidden(e, half)
+            for chunk in [slice(0, C)]:
+                silu(e, half, chunk)
+                quant_hidden(e, half, chunk)
 
-        def layer2(e, s):
+        def start_hidden(e, half):
+            flat = h_pool.tile([P, 4, C], BF16, name="h_flat", tag="h_flat", align_bytes=64)
+            h_laid = h_pool.tile([P, C, PACK], BF16, name="h_laid", tag="h_laid", align_bytes=64)
+            words = h_pool.tile([P, C], U32, name="h_words", tag=f"h_words{half}", align_bytes=64)
+            scales = h_pool.tile([P, C], U8, name="h_bytes", tag=f"h_bytes{half}", align_bytes=64)
+            h_codes[e, half] = (words, scales)
+            h_stage[e, half] = (flat, h_laid)
+
+        def silu(e, half, chunk):
+            flat = h_stage[e, half][0]
+            for t in range(4):
+                nc.scalar.activation(flat[:, t, chunk], accs[e, half, t][:, chunk], SILU)
+
+        def quant_hidden(e, half, chunk):
+            flat, h_laid = h_stage[e, half]
+            words, scales = h_codes[e, half]
+            nc.vector.tensor_copy(
+                h_laid[:, chunk, :].rearrange("p (c i) t -> p c t i", i=4),
+                flat[:, :, chunk].rearrange("p t (c i) -> p c t i", i=4),
+            )
+            nc.vector.quantize_mx(
+                out=words[:, chunk].bitcast(FP8X4),
+                scales=scales[:, chunk],
+                in_=h_laid[:, chunk, :].rearrange("p c t -> p (c t)"),
+            )
+
+        def finish_w2(e, s):
+            nc.vector.quantize_mx(
+                out=w2_words[e, s][:].bitcast(FP8X4),
+                scales=w2_bytes[e, s][:],
+                in_=laid["w2", e, s][:].rearrange("p c j -> p (c j)"),
+            )
+
+        def layer2(e, s, only=None):
+            words, scales = h_codes[e, s]
             for c, chunk in enumerate(chunks(e)):
+                if only is not None and c != only:
+                    continue
                 width = chunk.stop - chunk.start
-                words, scales = h_codes[e, s]
                 for b in range(NB):
                     if s == 0:
                         y_banks[e, c, b] = psum.tile([P, width], F32, name="bank", tag="bank")
                     n_cols = slice(b * P, (b + 1) * P)
                     nc.tensor.matmul_mx(
                         out=y_banks[e, c, b][:],
-                        lhsT=w2_words[e][s][:, n_cols].bitcast(FP8X4),
-                        lhsT_scale=w2_bytes[e][s][:, n_cols],
+                        lhsT=w2_words[e, s][:, n_cols].bitcast(FP8X4),
+                        lhsT_scale=w2_bytes[e, s][:, n_cols],
                         rhs=words[:, chunk].bitcast(FP8X4),
                         rhs_scale=scales[:, chunk],
                         start=(s == 0),
                         stop=(s == HALVES - 1),
                     )
-                if s == HALVES - 1:
-                    first = e * C + chunk.start
-                    for b in range(NB):
-                        y_sb = h_pool.tile([P, width], F32, name="y_sb", tag=f"y_sb{b}")
-                        nc.scalar.copy(y_sb[:], y_banks[e, c, b][:])
-                        nc.vector.tensor_tensor(
-                            windows[b][:].indirect(offsets[:, first // 16 : (first + width) // 16]),
-                            y_sb[:],
-                            gate_sb[:, first : first + width],
-                            MULT,
-                        )
 
-        steps = []
-        for s in range(PASSES):
-            steps.append((s // 2, lambda s=s: x_unit(s)))
+        def scatter(e, only=None):
+            for c, chunk in enumerate(chunks(e)):
+                if only is not None and c != only:
+                    continue
+                width = chunk.stop - chunk.start
+                first = e * C + chunk.start
+                for b in range(NB):
+                    y_sb = h_pool.tile([P, width], F32, name="y_sb", tag=f"y_sb{b}")
+                    nc.scalar.copy(y_sb[:], y_banks[e, c, b][:])
+                    nc.vector.tensor_tensor(
+                        windows[b][:].indirect(offsets[:, first // 16 : (first + width) // 16]),
+                        y_sb[:],
+                        gate_sb[:, first : first + width],
+                        MULT,
+                    )
+
+        def finish(unit):
+            kind = unit[0]
+            if kind == "x":
+                finish_x(unit[1])
+                if unit[1] == 1:
+                    broadcast_gate()
+                if unit[1] == PASSES - 1:
+                    gather(0)
+            elif kind == "w1":
+                e, s, half = unit[1:]
+                quant_w1(e, s, half)
+                layer1(e, s, half)
+                if e == 0 and s == 1 and half == HALVES - 1:
+                    gather(1)
+                if s == PASSES - 1:
+                    hidden(e, half)
+            else:
+                e, s = unit[1:]
+                finish_w2(e, s)
+                layer2(e, s)
+                if s == HALVES - 1:
+                    scatter(e)
+
+        items = [("x", 0), ("x", 1)]
+        units = [("x", s) for s in range(PASSES)]
         for e in range(E):
-            for s in range(PASSES):
-                for hh in range(HALVES):
-                    steps.append((2 + e * 5 + s, lambda e=e, s=s, hh=hh: w1_unit(e, s, hh)))
-            for s in range(HALVES):
-                steps.append((2 + e * 5 + 4, lambda e=e, s=s: w2_unit(e, s)))
+            items += [("w1", e, s) for s in range(PASSES)] + [("w2", e)]
+            units += [("w1", e, s, half) for s in range(PASSES) for half in range(HALVES)]
+            units += [("w2", e, s) for s in range(HALVES)]
 
         loaded = 0
-        waiting = None
-        for tile_index, make in steps:
-            while loaded < len(loads) and loaded < tile_index + RAW_BUFS:
-                loads[loaded]()
+        for i, unit in enumerate(units[: -(HALVES + 1)]):
+            item = ("x", unit[1] // 2) if unit[0] == "x" else unit[0:3] if unit[0] == "w1" else unit[0:2]
+            while loaded < len(items) and loaded < items.index(item) + RAW_BUFS:
+                load(items[loaded])
                 loaded += 1
-            lay, finish = make()
-            lay()
-            if waiting is not None:
-                waiting()
-            waiting = finish
-        waiting()
+            lay(unit)
+            if i > 0:
+                finish(units[i - 1])
+        e = E - 1
+        first, second = chunks(e)
+        lay(("w1", e, 3, 1))
+        finish(("w1", e, 3, 0))
+        quant_w1(e, 3, 1)
+        layer1(e, 3, 1)
+        lay(("w2", e, 0))
+        start_hidden(e, 1)
+        silu(e, 1, first)
+        finish_w2(e, 0)
+        lay(("w2", e, 1))
+        finish_w2(e, 1)
+        quant_hidden(e, 1, first)
+        for c in range(2):
+            layer2(e, 0, c)
+        layer2(e, 1, 0)
+        silu(e, 1, second)
+        quant_hidden(e, 1, second)
+        layer2(e, 1, 1)
+        scatter(e, 0)
+        scatter(e, 1)
 
         for b in range(NB):
             nc.sync.dma_start(out[b * P : (b + 1) * P, :], windows[b][:])

from contextlib import ExitStack

import concourse.mybir as mybir

K, T, E, C, H, N = 2048, 512, 2, 256, 1024, 256
FLOPS = 2 * E * C * (K * H + H * N)

F32 = mybir.dt.float32
BF16 = mybir.dt.bfloat16
U32 = mybir.dt.uint32
U16 = mybir.dt.uint16
U8 = mybir.dt.uint8
FP8X4 = mybir.dt.float8_e4m3fn_x4
MULT = mybir.AluOpType.mult
SILU = mybir.ActivationFunctionType.Silu

P = 128
PACK = 4
KP = P * PACK
PASSES = K // KP
HALVES = H // KP
NB = N // P
LIST = C // 16

RAW_BUFS = 6
V_X = 128
V_W1 = {(0, 0): 48, (0, 1): 48, (0, 2): 48, (0, 3): 48, (1, 0): 56, (1, 1): 56, (1, 2): 64, (1, 3): 64}
V_LAST = 72
V_W2 = {(0, 0): 0, (0, 1): 0, (1, 0): 128, (1, 1): 128}


def tile_routed_moe_kernel(tc, xT, w1, w2, gate, offs, out):
    nc = tc.nc
    x_rows = xT.rearrange("(s p j) t -> s p j t", p=P, j=PACK)
    w1_rows = w1.rearrange("e (s p j) i -> e s p j i", p=P, j=PACK)
    w2_rows = w2.rearrange("e (s p j) n -> e s p j n", p=P, j=PACK)

    with ExitStack() as ctx:
        keep = ctx.enter_context(tc.tile_pool(name="keep", bufs=1))
        raw_pool = ctx.enter_context(tc.tile_pool(name="raw_pool", bufs=RAW_BUFS))
        lay_pool = ctx.enter_context(tc.tile_pool(name="lay_pool", bufs=4))
        h_pool = ctx.enter_context(tc.tile_pool(name="h_pool", bufs=2))
        psum = ctx.enter_context(tc.psum_pool(name="psum", bufs=8))

        offsets = keep.tile([P, T // 16], U16, name="offsets")
        warm = keep.tile([P, 8], F32, name="warm")
        ones = keep.tile([P, P], F32, name="ones")
        gate_row = keep.tile([P, T], F32, name="gate_row")
        gate_sb = keep.tile([P, T], F32, name="gate_sb")
        x_words = keep.tile([P, PASSES, T], U32, name="x_words", align_bytes=64)
        x_bytes = keep.tile([P, T], U8, name="x_bytes", align_bytes=64)
        g_words = keep.tile([P, PASSES, T], U32, name="g_words", align_bytes=64)
        g_bytes = keep.tile([P, T], U8, name="g_bytes", align_bytes=64)
        windows = [keep.tile([P, T], F32, name=f"window{b}") for b in range(NB)]
        w1_words = {}
        w1_bytes = {}
        w2_words = {}
        w2_bytes = {}
        for e in range(E):
            for s in range(PASSES):
                w1_words[e, s] = keep.tile([P, H], U32, name=f"w1_words{e}{s}", align_bytes=64)
                w1_bytes[e, s] = keep.tile([P, H], U8, name=f"w1_bytes{e}{s}", align_bytes=64)
            for s in range(HALVES):
                w2_words[e, s] = keep.tile([P, N], U32, name=f"w2_words{e}{s}", align_bytes=64)
                w2_bytes[e, s] = keep.tile([P, N], U8, name=f"w2_bytes{e}{s}", align_bytes=64)

        nc.vector.memset(warm[:], 0.0)
        nc.scalar.activation(warm[:], warm[:], SILU)
        nc.gpsimd.memset(x_bytes[:], 0)
        nc.gpsimd.memset(gate_row[:], 0.0)
        nc.gpsimd.memset(ones[:], 1.0)

        raws = {}
        laid = {}
        accs = {}
        h_codes = {}
        h_stage = {}
        y_banks = {}

        def load(item):
            kind = item[0]
            if kind == "x":
                raw = raw_pool.tile([P, 2, PACK, T], F32, name="raw", tag="raw")
                for i in range(2):
                    nc.sync.dma_start(raw[:, i, :, :], x_rows[2 * item[1] + i])
                    if item[1] == 0 and i == 0:
                        nc.sync.dma_start(offsets[:], offs)
                        nc.sync.dma_start(gate_row[0:1, :], gate[0:1, :])
            elif kind == "w1":
                e, s = item[1:]
                raw = raw_pool.tile([P, PACK, H], F32, name="raw", tag="raw")
                if e == E - 1 and s == PASSES - 1:
                    nc.sync.dma_start(raw[:, :, 0:KP], w1_rows[e, s, :, :, 0:KP])
                    for j in range(0, PACK, 2):
                        nc.sync.dma_start(raw[:, j : j + 2, KP:H], w1_rows[e, s, :, j : j + 2, KP:H])
                else:
                    nc.sync.dma_start(raw[:], w1_rows[e, s])
            else:
                e = item[1]
                raw = raw_pool.tile([P, HALVES, PACK, N], F32, name="raw", tag="raw")
                for s in range(HALVES):
                    nc.sync.dma_start(raw[:, s, :, :], w2_rows[e, s])
            raws[item] = raw

        def lay_plain(dst, src, columns, split):
            if split > 0:
                nc.vector.tensor_copy(
                    dst[:, 0:split, :].rearrange("p (c i) j -> p c j i", i=4),
                    src[:, :, 0:split].rearrange("p j (c i) -> p c j i", i=4),
                )
            if split < columns:
                nc.scalar.copy(
                    dst[:, split:columns, :].rearrange("p (c i) j -> p c j i", i=4),
                    src[:, :, split:columns].rearrange("p j (c i) -> p c j i", i=4),
                )

        def lay_blocks(dst, src, split, js):
            for j in range(0, PACK, js):
                if split > 0:
                    nc.vector.tensor_copy(
                        dst[:, :, 0:split, j : j + js].rearrange("p t m j -> p m j t"),
                        src[:, j : j + js, 0 : 4 * split].rearrange("p j (m t) -> p m j t", t=4),
                    )
                if split < P:
                    nc.scalar.copy(
                        dst[:, :, split:P, j : j + js].rearrange("p t m j -> p m j t"),
                        src[:, j : j + js, 4 * split : KP].rearrange("p j (m t) -> p m j t", t=4),
                    )

        def lay(unit):
            kind = unit[0]
            if kind == "x":
                s = unit[1]
                tile = lay_pool.tile([P, T, PACK], BF16, name="laid", tag="laid", align_bytes=64)
                lay_plain(tile, raws["x", s // 2][:, s % 2, :, :], T, V_X)
            elif kind == "w1":
                e, s, half = unit[1:]
                tile = lay_pool.tile([P, 4, P, PACK], BF16, name="laid", tag="laid", align_bytes=64)
                last = e == E - 1 and s == PASSES - 1 and half == HALVES - 1
                lay_blocks(tile, raws["w1", e, s][:, :, half * KP : (half + 1) * KP], V_LAST if last else V_W1[e, s], 2 if last else PACK)
            else:
                e, s = unit[1:]
                tile = lay_pool.tile([P, N, PACK], BF16, name="laid", tag="laid", align_bytes=64)
                lay_plain(tile, raws["w2", e][:, s, :, :], N, V_W2[e, s])
            laid[unit] = tile

        def finish_x(s):
            nc.vector.quantize_mx(
                out=x_words[:, s, :].bitcast(FP8X4),
                scales=x_bytes[4 * s : P, :],
                in_=laid["x", s][:].rearrange("p c j -> p (c j)"),
            )

        def broadcast_gate():
            bank = psum.tile([P, T], F32, name="bank", tag="bank")
            nc.tensor.matmul(bank[:], ones[:], gate_row[:], start=True, stop=True)
            nc.scalar.copy(gate_sb[:], bank[:])

        def gather(e):
            columns = slice(e * C, (e + 1) * C)
            picked = offsets[:, e * LIST : (e + 1) * LIST]
            nc.vector.tensor_copy(g_bytes[:, columns], x_bytes[:].indirect(picked))
            for s in range(PASSES):
                nc.vector.tensor_copy(g_words[:, s, columns], x_words[:, s, :].indirect(picked))

        def quant_w1(e, s, half):
            pieces = (4 if half == HALVES - 1 else 1) if e == E - 1 and s == PASSES - 1 else 1
            for q in range(pieces):
                blocks = slice(q * 4 // pieces, (q + 1) * 4 // pieces)
                columns = slice(half * KP + blocks.start * P, half * KP + blocks.stop * P)
                nc.vector.quantize_mx(
                    out=w1_words[e, s][:, columns].bitcast(FP8X4),
                    scales=w1_bytes[e, s][:, columns],
                    in_=laid["w1", e, s, half][:, blocks, :, :].rearrange("p t m j -> p (t m j)"),
                )

        def layer1(e, s, half):
            parts = 1
            for n in range(parts):
                n_cols = slice(n * C // parts, (n + 1) * C // parts)
                g_cols = slice(e * C + n_cols.start, e * C + n_cols.stop)
                for t in range(4):
                    if s == 0:
                        accs[e, half, t] = psum.tile([P, C], F32, name="bank", tag="bank")
                    block = slice(half * KP + t * P, half * KP + (t + 1) * P)
                    nc.tensor.matmul_mx(
                        out=accs[e, half, t][:, n_cols],
                        lhsT=w1_words[e, s][:, block].bitcast(FP8X4),
                        lhsT_scale=w1_bytes[e, s][:, block],
                        rhs=g_words[:, s, g_cols].bitcast(FP8X4),
                        rhs_scale=g_bytes[4 * s : P, g_cols],
                        start=(s == 0),
                        stop=(s == PASSES - 1),
                    )

        def chunks(e):
            width = C if e == 0 else 128
            return [slice(c, c + width) for c in range(0, C, width)]

        def hidden(e, half):
            start_hidden(e, half)
            for chunk in [slice(0, C)]:
                silu(e, half, chunk)
                quant_hidden(e, half, chunk)

        def start_hidden(e, half):
            flat = h_pool.tile([P, 4, C], BF16, name="h_flat", tag="h_flat", align_bytes=64)
            h_laid = h_pool.tile([P, C, PACK], BF16, name="h_laid", tag="h_laid", align_bytes=64)
            words = h_pool.tile([P, C], U32, name="h_words", tag=f"h_words{half}", align_bytes=64)
            scales = h_pool.tile([P, C], U8, name="h_bytes", tag=f"h_bytes{half}", align_bytes=64)
            h_codes[e, half] = (words, scales)
            h_stage[e, half] = (flat, h_laid)

        def silu(e, half, chunk):
            flat = h_stage[e, half][0]
            for t in range(4):
                nc.scalar.activation(flat[:, t, chunk], accs[e, half, t][:, chunk], SILU)

        def quant_hidden(e, half, chunk):
            flat, h_laid = h_stage[e, half]
            words, scales = h_codes[e, half]
            nc.vector.tensor_copy(
                h_laid[:, chunk, :].rearrange("p (c i) t -> p c t i", i=4),
                flat[:, :, chunk].rearrange("p t (c i) -> p c t i", i=4),
            )
            nc.vector.quantize_mx(
                out=words[:, chunk].bitcast(FP8X4),
                scales=scales[:, chunk],
                in_=h_laid[:, chunk, :].rearrange("p c t -> p (c t)"),
            )

        def finish_w2(e, s):
            nc.vector.quantize_mx(
                out=w2_words[e, s][:].bitcast(FP8X4),
                scales=w2_bytes[e, s][:],
                in_=laid["w2", e, s][:].rearrange("p c j -> p (c j)"),
            )

        def layer2(e, s, only=None):
            words, scales = h_codes[e, s]
            for c, chunk in enumerate(chunks(e)):
                if only is not None and c != only:
                    continue
                width = chunk.stop - chunk.start
                for b in range(NB):
                    if s == 0:
                        y_banks[e, c, b] = psum.tile([P, width], F32, name="bank", tag="bank")
                    n_cols = slice(b * P, (b + 1) * P)
                    nc.tensor.matmul_mx(
                        out=y_banks[e, c, b][:],
                        lhsT=w2_words[e, s][:, n_cols].bitcast(FP8X4),
                        lhsT_scale=w2_bytes[e, s][:, n_cols],
                        rhs=words[:, chunk].bitcast(FP8X4),
                        rhs_scale=scales[:, chunk],
                        start=(s == 0),
                        stop=(s == HALVES - 1),
                    )

        def scatter(e, only=None):
            for c, chunk in enumerate(chunks(e)):
                if only is not None and c != only:
                    continue
                width = chunk.stop - chunk.start
                first = e * C + chunk.start
                for b in range(NB):
                    y_sb = h_pool.tile([P, width], F32, name="y_sb", tag=f"y_sb{b}")
                    nc.scalar.copy(y_sb[:], y_banks[e, c, b][:])
                    nc.vector.tensor_tensor(
                        windows[b][:].indirect(offsets[:, first // 16 : (first + width) // 16]),
                        y_sb[:],
                        gate_sb[:, first : first + width],
                        MULT,
                    )

        def finish(unit):
            kind = unit[0]
            if kind == "x":
                finish_x(unit[1])
                if unit[1] == 1:
                    broadcast_gate()
                if unit[1] == PASSES - 1:
                    gather(0)
            elif kind == "w1":
                e, s, half = unit[1:]
                quant_w1(e, s, half)
                layer1(e, s, half)
                if e == 0 and s == 1 and half == HALVES - 1:
                    gather(1)
                if s == PASSES - 1:
                    hidden(e, half)
            else:
                e, s = unit[1:]
                finish_w2(e, s)
                layer2(e, s)
                if s == HALVES - 1:
                    scatter(e)

        items = [("x", 0), ("x", 1)]
        units = [("x", s) for s in range(PASSES)]
        for e in range(E):
            items += [("w1", e, s) for s in range(PASSES)] + [("w2", e)]
            units += [("w1", e, s, half) for s in range(PASSES) for half in range(HALVES)]
            units += [("w2", e, s) for s in range(HALVES)]

        loaded = 0
        for i, unit in enumerate(units[: -(HALVES + 1)]):
            item = ("x", unit[1] // 2) if unit[0] == "x" else unit[0:3] if unit[0] == "w1" else unit[0:2]
            while loaded < len(items) and loaded < items.index(item) + RAW_BUFS:
                load(items[loaded])
                loaded += 1
            lay(unit)
            if i > 0:
                finish(units[i - 1])
        e = E - 1
        first, second = chunks(e)
        lay(("w1", e, 3, 1))
        finish(("w1", e, 3, 0))
        quant_w1(e, 3, 1)
        layer1(e, 3, 1)
        lay(("w2", e, 0))
        start_hidden(e, 1)
        silu(e, 1, first)
        finish_w2(e, 0)
        lay(("w2", e, 1))
        finish_w2(e, 1)
        quant_hidden(e, 1, first)
        for c in range(2):
            layer2(e, 0, c)
        layer2(e, 1, 0)
        silu(e, 1, second)
        quant_hidden(e, 1, second)
        layer2(e, 1, 1)
        scatter(e, 0)
        scatter(e, 1)

        for b in range(NB):
            nc.sync.dma_start(out[b * P : (b + 1) * P, :], windows[b][:])
